import numpy as np
import ml_dtypes


def mxq(x, axis, fmt="e4m3"):
    dtype, down = {"e4m3": (ml_dtypes.float8_e4m3fn, 7), "e5m2": (ml_dtypes.float8_e5m2, 14)}[fmt]
    v = np.moveaxis(np.asarray(x, np.float32).astype(ml_dtypes.bfloat16).astype(np.float64), axis, -1)
    blocks = v.reshape(v.shape[:-1] + (-1, 32))
    amax = np.abs(blocks).max(-1, keepdims=True)
    byte = np.maximum(np.where(amax > 0, np.frexp(amax)[1] - 1 + 127, 0) - down, 1)
    scale = np.exp2(byte - 127.0)
    codes = (blocks / scale).astype(np.float32).astype(dtype).astype(np.float64)
    return np.moveaxis((codes * scale).reshape(v.shape), -1, axis)


WIDE = False


def mx_kscale(k):
    if not WIDE:
        return np.ones(k)
    levels = np.array([10, -10, 5, -5, 0])
    if k % 512:
        return np.exp2(np.random.permutation(np.resize(levels, k // 32))).repeat(32)
    a = np.empty((k // 512, 16))
    for p in range(k // 512):
        a[p, :8] = np.random.permutation(np.resize(levels, 8))
        for g in range(8):
            far = levels[np.abs(levels - a[p, g]) >= 10]
            a[p, g + 8] = far[np.random.randint(len(far))]
    return np.exp2(a.ravel()).repeat(32)


BF16 = ml_dtypes.bfloat16


def bf(x):
    return np.asarray(x, np.float32).astype(BF16)


def f64(x):
    return np.asarray(x).astype(np.float64)


E2M1 = np.array([0.0, 0.5, 1.0, 1.5, 2.0, 3.0, 4.0, 6.0, -0.0, -0.5, -1.0, -1.5, -2.0, -3.0, -4.0, -6.0])


def pack_weight(w, fmt):
    k, n = w.shape
    w = f64(bf(w)).reshape(k // 32, 32, n)
    amax = np.abs(w).max(1)
    if fmt == "e4m3":
        byte = np.frexp(amax)[1] - 1 + 127 - 7
    else:
        mant, ex = np.frexp(amax / 6.0)
        byte = np.where(mant > 0.5, ex, ex - 1) + 127
    byte = np.clip(np.where(amax > 0, byte, 1), 1, 254)
    scaled = (w * np.exp2(127.0 - byte)[:, None, :]).reshape(k, n).astype(np.float32)
    by_word = np.ascontiguousarray(scaled.reshape(k // 512, 128, 4, n).transpose(0, 1, 3, 2))
    if fmt == "e4m3":
        words = by_word.astype(ml_dtypes.float8_e4m3fn).view(np.uint8)
    else:
        c = by_word.astype(ml_dtypes.float4_e2m1fn).view(np.uint8) & 0xF
        words = c[..., 0::2] | (c[..., 1::2] << 4)
    return np.ascontiguousarray(words), np.ascontiguousarray(byte.astype(np.uint8).reshape(k // 512, 16, n))


def unpack_weight(words, scales, fmt):
    g, p, n, _ = words.shape
    if fmt == "e4m3":
        vals = np.ascontiguousarray(words).view(ml_dtypes.float8_e4m3fn).astype(np.float64)
    else:
        nib = np.empty((g, p, n, 4), np.uint8)
        nib[..., 0::2] = words & 0xF
        nib[..., 1::2] = words >> 4
        vals = E2M1[nib]
    vals = vals * np.repeat(np.exp2(scales.astype(np.float64) - 127.0), 8, axis=1)[..., None]
    return vals.transpose(0, 1, 3, 2).reshape(g * 512, n)
def pack4(w):
    words, scales = pack_weight(w, "e2m1")
    return words.reshape(words.shape[0], 128, -1), scales


def unpack4(words, scales):
    return unpack_weight(words.reshape(words.shape[0], 128, -1, 2), scales, "e2m1")


def planes(Y):
    n, m = Y.shape
    b = f64(bf(Y)).reshape(n // 32, 32, m)
    amax = np.abs(b).max(1)
    byte = np.clip(np.where(amax > 0, np.frexp(amax)[1] - 1 + 127 - 7, 1), 1, 254)
    codes = (b * np.exp2(127.0 - byte)[:, None, :]).reshape(n, m).astype(np.float32).astype(ml_dtypes.float8_e4m3fn).view(np.uint8)
    words = codes.reshape(n // 512, 128, 4, m).transpose(0, 1, 3, 2)
    return np.ascontiguousarray(words), np.ascontiguousarray(byte.astype(np.uint8).reshape(n // 512, 16, m))


M, K, N = 1024, 1536, 2048

TOKEN_SPREAD = 0.3
CHANNEL_SPREAD = 0.8
BIAS = 0.3
FLOOR = 0.5


def setup_inputs():
    s = mx_kscale(K)
    x = np.random.randn(M, K) * s[None, :]
    w = np.random.randn(K, N) / np.sqrt(K) / s[:, None]
    w_words, w_scales = pack4(w)
    token_scale = np.exp(TOKEN_SPREAD * np.random.randn(M))
    channel_scale = np.exp(CHANNEL_SPREAD * np.random.randn(N))
    bias = BIAS * channel_scale * np.random.randn(N)
    floor_value = -FLOOR * channel_scale * np.exp(0.1 * np.random.randn(N))
    return {"x": bf(x), "w_words": w_words, "w_scales": w_scales,
            "token_scale": bf(token_scale), "channel_scale": bf(channel_scale),
            "bias": bf(bias), "floor_value": bf(floor_value)}


def reference(x, w_words, w_scales, token_scale, channel_scale, bias, floor_value):
    xq = mxq(f64(x), 1, "e4m3")
    w = unpack4(w_words, w_scales)
    acc = xq @ w
    z = acc * f64(token_scale)[:, None] * f64(channel_scale)[None, :] + f64(bias)[None, :]
    y = np.maximum(z, f64(floor_value)[None, :])
    Y = y.T
    words, scales = planes(Y)
    return y, words, scales

@@ -1,0 +1,330 @@
+from contextlib import ExitStack
+
+import concourse.mybir as mybir
+from concourse.masks import make_identity
+
+M, K, N = 1024, 1536, 2048
+FLOPS = 2 * M * K * N
+
+F32 = mybir.dt.float32
+BF16 = mybir.dt.bfloat16
+I32 = mybir.dt.int32
+U32 = mybir.dt.uint32
+U8 = mybir.dt.uint8
+FP8X4 = mybir.dt.float8_e4m3fn_x4
+FP4X4 = mybir.dt.float4_e2m1fn_x4
+ALU = mybir.AluOpType
+
+P = 128
+
+BLOCKS = [(0, 0), (1, 0), (0, 1), (1, 1), (2, 0), (2, 1), (3, 0), (3, 1)]
+
+
+def schedule(vshare=(0, 0, 0, 0, 0, 128, 256, 512), turn_after=2):
+    ops = []
+    add = lambda *op: ops.append(op)
+    add("setup")
+    for op in [("load_w", 0), ("load_ws",), ("load_x", 0, 0), ("load_x", 0, 1), ("load_x", 0, 2), ("load_w", 1), ("load_x", 1, 0), ("load_x", 1, 1), ("load_x", 1, 2), ("load_w", 2), ("load_w", 3)]:
+        add(*op)
+    add("spread_ts")
+    for t in range(4):
+        add("perm_c", 0, t)
+    for g in range(4):
+        add("perm_s", g)
+    for kg in range(3):
+        add("turn_x", 0, kg)
+        add("copy_x", 0, kg)
+    add("quant_x", 0, 0)
+    add("quant_x", 0, 1)
+    add("perm_c", 1, 0)
+    add("quant_x", 0, 2)
+    for kg in range(2):
+        for t in range(4):
+            add("mx", 0, t, kg)
+    add("perm_c", 1, 1)
+    add("perm_c", 1, 2)
+    fills = {
+        0: [[("perm_c", 1, 3)], [], []],
+        1: [[("quant_x", 1, 0)], [("quant_x", 1, 1)], [("quant_x", 1, 2)]],
+        2: [[("quant_y", 0)], [("perm_c", 2, 0)], [("perm_c", 2, 1)]],
+        3: [[("perm_c", 2, 2)], [("perm_c", 2, 3)], []],
+        4: [[("perm_c", 3, 0)], [("perm_c", 3, 1)], []],
+        5: [[("perm_c", 3, 2)], [("perm_c", 3, 3)], []],
+        6: [[], [], []], 7: [[], [], []]}
+    def out_y(s):
+        add("turn_y", s, range(4), range(4))
+        for j in range(4):
+            add("copy_y", s, j, "S")
+            add("store_y", s, j, j + 1)
+    for s in range(8):
+        last = s == 7
+        if s >= 1:
+            v = vshare[s - 1]
+        for t in range(4):
+            for kg in range(3) if s else [2]:
+                add("mx", s, t, kg)
+            if s == 0 and t == 3:
+                for kg in range(2):
+                    add("turn_x", 1, kg)
+                    add("copy_x", 1, kg)
+            if s == 1:
+                if t == 1:
+                    add("turn_x", 1, 2)
+                    add("copy_x", 1, 2)
+                    add("weave", 0, 0, 512, "S")
+                if t == 3:
+                    out_y(0)
+            elif s >= 2 and t == 0:
+                add("weave", s - 1, v, 512, "S")
+            if s >= 2 and t == (1 if last else turn_after):
+                out_y(s - 1)
+            add("scale", s, t)
+            if t >= 1:
+                add("clamp", s, t - 1)
+            if t == 0 and s >= 2 and v:
+                add("weave", s - 1, 0, v, "V")
+            if t < 3:
+                for op in fills[s][t]:
+                    add(*op)
+                    if op[0] == "quant_y":
+                        add("store_q", op[1])
+                if t == 2 and s >= 2:
+                    add("quant_y", s - 1)
+                    add("store_q", s - 1)
+                    if last:
+                        add("store_s", 0, 3)
+        if last:
+            add("turn_y", s, range(4), range(3))
+        add("clamp", s, 3)
+    add("turn_y", 7, range(4), [3])
+    add("weave", 7, 0, 512, "V")
+    for j in range(3):
+        add("copy_y", 7, j, "S")
+        add("store_y", 7, j, j + 1)
+    add("quant_y", 7)
+    add("store_q", 7)
+    add("store_s", 3, 4)
+    add("copy_y", 7, 3, "S")
+    add("store_y", 7, 3, 4)
+    return ops
+
+
+def tile_dequant_linear_shifted_relu_g4_kernel(
+    tc, x, w_words, w_scales, token_scale, channel_scale, bias, floor_value, out_0, out_1, out_2
+):
+    nc = tc.nc
+    with ExitStack() as ctx:
+        keep = ctx.enter_context(tc.tile_pool(name="keep", bufs=1))
+        work = ctx.enter_context(tc.tile_pool(name="work", bufs=4))
+        psum = ctx.enter_context(tc.psum_pool(name="psum", bufs=1))
+        ctx.enter_context(tc.manual_schedule())
+
+        ident = keep.tile([P, P], F32, name="ident")
+        ident_bf = keep.tile([P, P], BF16, name="ident_bf")
+        ts_col = keep.tile([P, 8], BF16, name="ts_col")
+        ts_all = keep.tile([P, M], BF16, name="ts_all")
+        vec_rows = keep.tile([P, 512], BF16, name="vec_rows")
+        vec_cols = keep.tile([P, 4, 12], F32, name="vec_cols")
+        ws_raw = keep.tile([P, 3, N], U8, name="ws_raw", align_bytes=64)
+        y_scales = keep.tile([P, 4, M], U8, name="y_scales", align_bytes=64)
+        w_raw = [keep.tile([P, 3 * 1024], U8, name=f"w_raw{g}", align_bytes=64) for g in range(4)]
+        w_codes = [keep.tile([P, 4, 3, 256], U8, name=f"w_codes{g}", align_bytes=64) for g in range(4)]
+        w_planes = [keep.tile([P, 4, 3, P], U8, name=f"w_planes{g}", align_bytes=64) for g in range(4)]
+        x_raw, x_codes, x_planes = {}, {}, {}
+        for h in range(2):
+            for kg in range(3):
+                x_raw[h, kg] = keep.tile([P, 4, 512], BF16, name=f"x_raw{h}{kg}", align_bytes=64)
+                x_codes[h, kg] = keep.tile([P, 512], U32, name=f"x_codes{h}{kg}", align_bytes=64)
+                x_planes[h, kg] = keep.tile([P, 512], U8, name=f"x_planes{h}{kg}", align_bytes=64)
+
+        tiles = {}
+        turns = []
+
+        def turn_bank(shape, dtype):
+            tag = f"turn{len(turns) % 4}"
+            turns.append(tag)
+            return psum.tile(shape, dtype, name=f"bank{len(turns)}", tag=tag)
+
+        def copy_on(engine, out, in_):
+            if engine == "S":
+                nc.scalar.copy(out=out, in_=in_)
+            else:
+                nc.vector.tensor_copy(out=out, in_=in_)
+
+        def setup():
+            ws_words = ws_raw[:].rearrange("p k n -> p (k n)").bitcast(I32)
+            nc.vector.memset(ws_words, 0)
+            make_identity(nc, ident[:])
+            nc.gpsimd.dma_start(out=ts_col[:], in_=token_scale.rearrange("(p j) -> p j", j=8))
+            nc.gpsimd.memset(vec_rows[:], 0.0)
+            for i, vec in enumerate((channel_scale, bias, floor_value)):
+                nc.gpsimd.dma_start(out=vec_rows[4 * i : 4 * i + 4, :], in_=vec.rearrange("(g c) -> g c", g=4))
+            nc.scalar.copy(out=ident_bf[:], in_=ident[:])
+
+        def load_x(h, kg):
+            rows = x[512 * h : 512 * (h + 1), 512 * kg : 512 * (kg + 1)]
+            nc.sync.dma_start(out=x_raw[h, kg][:], in_=rows.rearrange("(j p) k -> p j k", p=P))
+
+        def load_ws():
+            src = w_scales.bitcast(I32)
+            dst = ws_raw[:].bitcast(I32)
+            for q in range(4):
+                nc.sync.dma_start(
+                    out=dst[32 * q : 32 * q + 4, :, :],
+                    in_=src[:, 4 * q : 4 * q + 4, :].rearrange("k r n -> r k n"),
+                )
+
+        def load_w(g):
+            src = w_words.bitcast(I32)[:, :, 256 * g : 256 * (g + 1)]
+            dst = w_raw[g][:].bitcast(I32).rearrange("p (k n) -> p k n", k=3)
+            nc.sync.dma_start(out=dst, in_=src.rearrange("k p n -> p k n"))
+
+        def spread_ts():
+            bank = turn_bank([P, 8, P], BF16)
+            for j in range(8):
+                nc.tensor.transpose(bank[:, j, :], ts_col[:, j : j + 1].to_broadcast([P, P]), ident_bf[:])
+            nc.scalar.copy(
+                out=ts_all[:].rearrange("p (r j) -> p r j", j=8), in_=bank[:].rearrange("p j r -> p r j")
+            )
+            bank = turn_bank([P, 4, P], BF16)
+            for t in range(4):
+                nc.tensor.transpose(bank[:, t, :], vec_rows[:, t:512:4], ident_bf[:])
+            nc.scalar.copy(out=vec_cols[:], in_=bank[:, :, 0:12])
+
+        def turn_x(h, kg):
+            words = x_raw[h, kg][:].bitcast(F32)
+            for pair in range(2):
+                bank = turn_bank([P, 2, 2, P], F32)
+                tiles["xt", h, kg, pair] = bank
+                for j in range(2):
+                    for u in range(2):
+                        nc.tensor.transpose(bank[:, j, u, :], words[:, 2 * pair + j, u:256:2], ident[:])
+
+        def copy_x(h, kg, engine="S"):
+            grouped = work.tile([P, 2048], BF16, name="x_grouped", align_bytes=64)
+            tiles["xg", h, kg] = grouped
+            words = grouped[:].bitcast(F32)
+            for pair in range(2):
+                copy_on(
+                    engine,
+                    words[:, 512 * pair : 512 * (pair + 1)].rearrange("p (j r u) -> p j r u", j=2, u=2),
+                    tiles["xt", h, kg, pair][:].rearrange("p j u r -> p j r u"),
+                )
+
+        def quant_x(h, kg):
+            nc.vector.quantize_mx(
+                out=x_codes[h, kg][:].bitcast(FP8X4), scales=x_planes[h, kg][:], in_=tiles["xg", h, kg][:]
+            )
+
+        def perm_s(g):
+            src = ws_raw[:, :, 512 * g : 512 * (g + 1)].rearrange("p k (m t) -> p t k m", t=4)
+            nc.vector.tensor_copy(out=w_planes[g][:], in_=src)
+
+        def perm_c(g, t):
+            src = w_raw[g][:].rearrange("p (c t b) -> p t c b", t=4, b=2)[:, t, :, :]
+            dst = w_codes[g][:, t, :, :].rearrange("p k (m b) -> p (k m) b", b=2)
+            nc.vector.tensor_copy(out=dst, in_=src)
+
+        def mx(s, t, kg):
+            g, h = BLOCKS[s]
+            if kg == 0:
+                tiles["acc", s, t] = psum.tile([P, 512], F32, name=f"acc{s}{t}", tag=f"acc{t}")
+            nc.tensor.matmul_mx(
+                out=tiles["acc", s, t][:],
+                lhsT=w_codes[g][:, t, kg, :].bitcast(FP4X4),
+                lhsT_scale=w_planes[g][:, t, kg, :],
+                rhs=x_codes[h, kg][:].bitcast(FP8X4),
+                rhs_scale=x_planes[h, kg][:],
+                start=(kg == 0),
+                stop=(kg == 2),
+            )
+
+        def scale(s, t):
+            g, h = BLOCKS[s]
+            scaled = work.tile([P, 512], F32, name="scaled", bufs=6)
+            tiles["v", s, t] = scaled
+            nc.vector.scalar_tensor_tensor(
+                out=scaled[:],
+                in0=tiles["acc", s, t][:],
+                scalar=vec_cols[:, t, g : g + 1],
+                in1=ts_all[:, 512 * h : 512 * (h + 1)],
+                op0=ALU.mult,
+                op1=ALU.mult,
+            )
+
+        def clamp(s, t):
+            g, h = BLOCKS[s]
+            if t == 0:
+                tiles["y", s] = work.tile([P, 4, 512], F32, name="y_turned")
+            nc.vector.tensor_scalar(
+                out=tiles["y", s][:, t, :],
+                in0=tiles["v", s, t][:],
+                scalar1=vec_cols[:, t, 4 + g : 5 + g],
+                scalar2=vec_cols[:, t, 8 + g : 9 + g],
+                op0=ALU.add,
+                op1=ALU.max,
+            )
+
+        def weave(s, lo, hi, engine):
+            if ("yb", s) not in tiles:
+                tiles["yb", s] = work.tile([P, 2048], BF16, name="y_grouped", align_bytes=64)
+            dst = tiles["yb", s][:, 4 * lo : 4 * hi].rearrange("p (c i t) -> p c t i", i=4, t=4)
+            src = tiles["y", s][:, :, lo:hi].rearrange("p t (c i) -> p c t i", i=4)
+            copy_on(engine, dst, src)
+
+        def quant_y(s):
+            g, h = BLOCKS[s]
+            codes = work.tile([P, 512], U32, name="y_codes", align_bytes=64)
+            tiles["yq", s] = codes
+            nc.vector.quantize_mx(
+                out=codes[:].bitcast(FP8X4),
+                scales=y_scales[:, g, 512 * h : 512 * (h + 1)],
+                in_=tiles["yb", s][:],
+            )
+
+        def store_q(s):
+            g, h = BLOCKS[s]
+            dst = out_1[g].rearrange("p m t -> p (m t)").bitcast(I32)[:, 512 * h : 512 * (h + 1)]
+            nc.sync.dma_start(out=dst, in_=tiles["yq", s][:].bitcast(I32))
+
+        def store_s(lo, hi):
+            dst = out_2.bitcast(I32)
+            src = y_scales[:].bitcast(I32)
+            for q in range(4):
+                nc.sync.dma_start(
+                    out=dst[lo:hi, 4 * q : 4 * q + 4, :].rearrange("g r m -> r g m"),
+                    in_=src[32 * q : 32 * q + 4, lo:hi, :],
+                )
+
+        def turn_y(s, js, ts):
+            for j in js:
+                if ("yt", s, j) not in tiles:
+                    tiles["yt", s, j] = turn_bank([P, 4, P], F32)
+                for t in ts:
+                    nc.tensor.transpose(
+                        tiles["yt", s, j][:, t, :], tiles["y", s][:, t, P * j : P * (j + 1)], ident[:]
+                    )
+
+        def copy_y(s, j, engine):
+            rows = work.tile([P, 512], F32, name="y_rows", bufs=12)
+            tiles["yo", s, j] = rows
+            copy_on(
+                engine,
+                rows[:].rearrange("p (c t) -> p c t", t=4),
+                tiles["yt", s, j][:].rearrange("p t c -> p c t"),
+            )
+
+        def store_y(s, lo, hi):
+            g, h = BLOCKS[s]
+            for j in range(lo, hi):
+                row0 = 512 * h + P * j
+                nc.sync.dma_start(out=out_0[row0 : row0 + P, 512 * g : 512 * (g + 1)], in_=tiles["yo", s, j][:])
+
+        steps = dict(
+            setup=setup, load_x=load_x, load_ws=load_ws, load_w=load_w, spread_ts=spread_ts, turn_x=turn_x,
+            copy_x=copy_x, quant_x=quant_x, perm_s=perm_s, perm_c=perm_c, mx=mx, scale=scale, clamp=clamp,
+            weave=weave, quant_y=quant_y, store_q=store_q, store_s=store_s, turn_y=turn_y, copy_y=copy_y,
+            store_y=store_y,
+        )
+        for op in schedule():
+            steps[op[0]](*op[1:])

@@ -24,7 +24,7 @@ def schedule(vshare=(0, 0, 0, 0, 0, 128, 256, 512), turn_after=2):
     ops = []
     add = lambda *op: ops.append(op)
     add("setup")
-    for op in [("load_w", 0), ("load_ws",), ("load_x", 0, 0), ("load_x", 0, 1), ("load_x", 0, 2), ("load_w", 1), ("load_x", 1, 0), ("load_x", 1, 1), ("load_x", 1, 2), ("load_w", 2), ("load_w", 3)]:
+    for op in [("load_w", 0), ("load_x", 0, 0), ("load_vec",), ("load_ws",), ("load_x", 0, 1), ("load_x", 0, 2), ("load_w", 1), ("load_x", 1, 0), ("load_x", 1, 1), ("load_x", 1, 2), ("load_w", 2), ("load_w", 3)]:
         add(*op)
     add("spread_ts")
     for t in range(4):
@@ -91,10 +91,11 @@ def schedule(vshare=(0, 0, 0, 0, 0, 128, 256, 512), turn_after=2):
                 if t == 2 and s >= 2:
                     add("quant_y", s - 1)
                     add("store_q", s - 1)
-                    if last:
+                    if s == 6:
                         add("store_s", 0, 3)
         if last:
-            add("turn_y", s, range(4), range(3))
+            for t in range(3):
+                add("turn_y", s, range(4), [t])
         add("clamp", s, 3)
     add("turn_y", 7, range(4), [3])
     add("weave", 7, 0, 512, "V")
@@ -152,14 +153,16 @@ def tile_dequant_linear_shifted_relu_g4_kernel(
                 nc.vector.tensor_copy(out=out, in_=in_)
 
         def setup():
+            nc.vector.memset(vec_rows[:], 0.0)
             ws_words = ws_raw[:].rearrange("p k n -> p (k n)").bitcast(I32)
             nc.vector.memset(ws_words, 0)
             make_identity(nc, ident[:])
-            nc.gpsimd.dma_start(out=ts_col[:], in_=token_scale.rearrange("(p j) -> p j", j=8))
-            nc.gpsimd.memset(vec_rows[:], 0.0)
-            for i, vec in enumerate((channel_scale, bias, floor_value)):
-                nc.gpsimd.dma_start(out=vec_rows[4 * i : 4 * i + 4, :], in_=vec.rearrange("(g c) -> g c", g=4))
             nc.scalar.copy(out=ident_bf[:], in_=ident[:])
+
+        def load_vec():
+            nc.scalar.dma_start(out=ts_col[:], in_=token_scale.rearrange("(p j) -> p j", j=8))
+            for i, vec in enumerate((channel_scale, bias, floor_value)):
+                nc.scalar.dma_start(out=vec_rows[4 * i : 4 * i + 4, :], in_=vec.rearrange("(g c) -> g c", g=4))
 
         def load_x(h, kg):
             rows = x[512 * h : 512 * (h + 1), 512 * kg : 512 * (kg + 1)]
@@ -321,7 +324,7 @@ def tile_dequant_linear_shifted_relu_g4_kernel(
                 nc.sync.dma_start(out=out_0[row0 : row0 + P, 512 * g : 512 * (g + 1)], in_=tiles["yo", s, j][:])
 
         steps = dict(
-            setup=setup, load_x=load_x, load_ws=load_ws, load_w=load_w, spread_ts=spread_ts, turn_x=turn_x,
+            setup=setup, load_vec=load_vec, load_x=load_x, load_ws=load_ws, load_w=load_w, spread_ts=spread_ts, turn_x=turn_x,
             copy_x=copy_x, quant_x=quant_x, perm_s=perm_s, perm_c=perm_c, mx=mx, scale=scale, clamp=clamp,
             weave=weave, quant_y=quant_y, store_q=store_q, store_s=store_s, turn_y=turn_y, copy_y=copy_y,
             store_y=store_y,

@@ -20,46 +20,58 @@ P = 128
 BLOCKS = [(0, 0), (1, 0), (0, 1), (1, 1), (2, 0), (2, 1), (3, 0), (3, 1)]
 
 
-def schedule(vshare=(0, 0, 0, 0, 0, 128, 256, 512), turn_after=2):
+def schedule(vshare=(0, 0, 0, 0, 0, 128, 256), turn_after=(3, 2, 2, 2, 2, 2, 1), tmajor=(0, 0, 0, 0, 0, 0, 0),
+             wfirst=(1, 1, 1, 1, 1, 1, 1), qpos=(4, 2, 2, 2, 2, 2, 1), vpos=(0, 0, 0, 0, 0, 0, 0), last_v=512, last_eng="SSSS", reorder=0):
     ops = []
     add = lambda *op: ops.append(op)
     add("setup")
-    for op in [("load_w", 0), ("load_x", 0, 0), ("load_vec",), ("load_ws",), ("load_x", 0, 1), ("load_x", 0, 2), ("load_w", 1), ("load_x", 1, 0), ("load_x", 1, 1), ("load_x", 1, 2), ("load_w", 2), ("load_w", 3)]:
+    for op in [("load_vec",), ("load_w", 0), ("load_x", 0, 0), ("load_ws",), ("load_x", 0, 1), ("load_x", 0, 2), ("load_w", 1), ("load_x", 1, 0), ("load_x", 1, 1), ("load_x", 1, 2), ("load_w", 2), ("load_w", 3)]:
         add(*op)
+    add("warm_quant")
     add("spread_ts")
+    add("warm", 10)
     for t in range(4):
         add("perm_c", 0, t)
-    for g in range(4):
-        add("perm_s", g)
-    for kg in range(3):
-        add("turn_x", 0, kg)
-        add("copy_x", 0, kg)
+    add("perm_s", 0)
+    add("turn_x", 0, 0)
+    add("copy_x", 0, 0)
+    add("spread_vec")
+    add("warm", 4)
     add("quant_x", 0, 0)
+    add("perm_s", 1)
+    add("turn_x", 0, 1)
+    add("copy_x", 0, 1)
+    add("perm_s", 2)
     add("quant_x", 0, 1)
+    for t in range(4):
+        add("mx", 0, t, 0)
+    add("turn_x", 0, 2)
+    add("copy_x", 0, 2)
     add("perm_c", 1, 0)
-    add("quant_x", 0, 2)
-    for kg in range(2):
-        for t in range(4):
-            add("mx", 0, t, kg)
     add("perm_c", 1, 1)
+    add("quant_x", 0, 2)
+    for t in range(4):
+        add("mx", 0, t, 1)
     add("perm_c", 1, 2)
+    if reorder:
+        add("pair_x", 1, 0)
+        add("pair_x", 1, 1)
     fills = {
-        0: [[("perm_c", 1, 3)], [], []],
-        1: [[("quant_x", 1, 0)], [("quant_x", 1, 1)], [("quant_x", 1, 2)]],
-        2: [[("quant_y", 0)], [("perm_c", 2, 0)], [("perm_c", 2, 1)]],
-        3: [[("perm_c", 2, 2)], [("perm_c", 2, 3)], []],
-        4: [[("perm_c", 3, 0)], [("perm_c", 3, 1)], []],
-        5: [[("perm_c", 3, 2)], [("perm_c", 3, 3)], []],
-        6: [[], [], []], 7: [[], [], []]}
-    def out_y(s):
-        add("turn_y", s, range(4), range(4))
-        for j in range(4):
-            add("copy_y", s, j, "S")
-            add("store_y", s, j, j + 1)
+        0: [[("perm_c", 1, 3)], [], [("perm_s", 3)], []],
+        1: [[("quant_x", 1, 0)], [("quant_x", 1, 1)], [("quant_x", 1, 2)], []],
+        2: [[], [("perm_c", 2, 0)], [("perm_c", 2, 1)], []],
+        3: [[("perm_c", 2, 2)], [("perm_c", 2, 3)], [], []],
+        4: [[("perm_c", 3, 0)], [("perm_c", 3, 1)], [], []],
+        5: [[("perm_c", 3, 2)], [("perm_c", 3, 3)], [], []],
+        6: [[], [], [], []], 7: [[], [], [], []]}
+    def quant_out(s):
+        add("quant_y", s)
+        add("store_q", s)
+        if s == 5:
+            add("store_s", 0, 3)
     for s in range(8):
         last = s == 7
-        if s >= 1:
-            v = vshare[s - 1]
+        r = s - 1
         for t in range(4):
             for kg in range(3) if s else [2]:
                 add("mx", s, t, kg)
@@ -67,46 +79,56 @@ def schedule(vshare=(0, 0, 0, 0, 0, 128, 256, 512), turn_after=2):
                 for kg in range(2):
                     add("turn_x", 1, kg)
                     add("copy_x", 1, kg)
-            if s == 1:
-                if t == 1:
-                    add("turn_x", 1, 2)
-                    add("copy_x", 1, 2)
-                    add("weave", 0, 0, 512, "S")
-                if t == 3:
-                    out_y(0)
-            elif s >= 2 and t == 0:
-                add("weave", s - 1, v, 512, "S")
-            if s >= 2 and t == (1 if last else turn_after):
-                out_y(s - 1)
+                if reorder:
+                    add("pair_x", 1, 2)
+            if s == 1 and t == 1:
+                add("turn_x", 1, 2)
+                add("copy_x", 1, 2)
+            if s >= 1:
+                if wfirst[r] and t == (1 if s == 1 else 0) and vshare[r] < 512:
+                    add("weave", r, vshare[r], 512, "S")
+                if t == turn_after[r]:
+                    if tmajor[r]:
+                        for u in range(4):
+                            add("turn_y", r, range(4), [u])
+                    else:
+                        add("turn_y", r, range(4), range(4))
+                    for j in range(4):
+                        add("copy_y", r, j, "S")
+                        if j % 2:
+                            add("store_y", r, j - 1, j + 1)
+                    if not wfirst[r] and vshare[r] < 512:
+                        add("weave", r, vshare[r], 512, "S")
             add("scale", s, t)
             if t >= 1:
                 add("clamp", s, t - 1)
-            if t == 0 and s >= 2 and v:
-                add("weave", s - 1, 0, v, "V")
-            if t < 3:
-                for op in fills[s][t]:
-                    add(*op)
-                    if op[0] == "quant_y":
-                        add("store_q", op[1])
-                if t == 2 and s >= 2:
-                    add("quant_y", s - 1)
-                    add("store_q", s - 1)
-                    if s == 6:
-                        add("store_s", 0, 3)
-        if last:
-            for t in range(3):
-                add("turn_y", s, range(4), [t])
+            if s >= 1 and t == vpos[r] and vshare[r]:
+                add("weave", r, 0, vshare[r], "V")
+            for op in fills[s][t]:
+                add(*op)
+            if s >= 2 and qpos[s - 2] == 4 + t:
+                quant_out(s - 2)
+            if s >= 1 and qpos[r] == t:
+                quant_out(r)
+            if t == 3 and last:
+                for u in range(3):
+                    add("turn_y", s, range(4), [u])
         add("clamp", s, 3)
     add("turn_y", 7, range(4), [3])
-    add("weave", 7, 0, 512, "V")
+    if qpos[6] == 4:
+        quant_out(6)
+    add("weave", 7, 0, last_v, "V")
+    if last_v < 512:
+        add("weave", 7, last_v, 512, "S")
     for j in range(3):
-        add("copy_y", 7, j, "S")
-        add("store_y", 7, j, j + 1)
+        add("copy_y", 7, j, last_eng[j])
+        if j:
+            add("store_y", 7, 0 if j == 1 else j, j + 1)
     add("quant_y", 7)
     add("store_q", 7)
-    add("store_s", 3, 4)
-    add("copy_y", 7, 3, "S")
+    add("copy_y", 7, 3, last_eng[3])
     add("store_y", 7, 3, 4)
+    add("store_s", 3, 4)
     return ops
 
 
@@ -124,7 +146,9 @@ def tile_dequant_linear_shifted_relu_g4_kernel(
         ident_bf = keep.tile([P, P], BF16, name="ident_bf")
         ts_col = keep.tile([P, 8], BF16, name="ts_col")
         ts_all = keep.tile([P, M], BF16, name="ts_all")
-        vec_rows = keep.tile([P, 512], BF16, name="vec_rows")
+        vec_rows = keep.tile([P, 512], BF16, name="vec_rows", align_bytes=64)
+        warm_codes = keep.tile([P, P], U32, name="warm_codes", align_bytes=64)
+        warm_plane = keep.tile([P, P], U8, name="warm_plane", align_bytes=64)
         vec_cols = keep.tile([P, 4, 12], F32, name="vec_cols")
         ws_raw = keep.tile([P, 3, N], U8, name="ws_raw", align_bytes=64)
         y_scales = keep.tile([P, 4, M], U8, name="y_scales", align_bytes=64)
@@ -157,7 +181,7 @@ def tile_dequant_linear_shifted_relu_g4_kernel(
             ws_words = ws_raw[:].rearrange("p k n -> p (k n)").bitcast(I32)
             nc.vector.memset(ws_words, 0)
             make_identity(nc, ident[:])
-            nc.scalar.copy(out=ident_bf[:], in_=ident[:])
+            nc.vector.tensor_copy(out=ident_bf[:], in_=ident[:])
 
         def load_vec():
             nc.scalar.dma_start(out=ts_col[:], in_=token_scale.rearrange("(p j) -> p j", j=8))
@@ -189,10 +213,18 @@ def tile_dequant_linear_shifted_relu_g4_kernel(
             nc.scalar.copy(
                 out=ts_all[:].rearrange("p (r j) -> p r j", j=8), in_=bank[:].rearrange("p j r -> p r j")
             )
+
+        def spread_vec():
             bank = turn_bank([P, 4, P], BF16)
             for t in range(4):
                 nc.tensor.transpose(bank[:, t, :], vec_rows[:, t:512:4], ident_bf[:])
             nc.scalar.copy(out=vec_cols[:], in_=bank[:, :, 0:12])
+
+        def pair_x(h, kg):
+            paired = work.tile([P, 4, 2, P], F32, name="x_paired", bufs=3)
+            tiles["xp", h, kg] = paired
+            words = x_raw[h, kg][:].bitcast(F32)
+            nc.scalar.copy(out=paired[:], in_=words.rearrange("p j (c u) -> p j u c", u=2))
 
         def turn_x(h, kg):
             words = x_raw[h, kg][:].bitcast(F32)
@@ -201,7 +233,11 @@ def tile_dequant_linear_shifted_relu_g4_kernel(
                 tiles["xt", h, kg, pair] = bank
                 for j in range(2):
                     for u in range(2):
-                        nc.tensor.transpose(bank[:, j, u, :], words[:, 2 * pair + j, u:256:2], ident[:])
+                        if ("xp", h, kg) in tiles:
+                            src = tiles["xp", h, kg][:, 2 * pair + j, u, :]
+                        else:
+                            src = words[:, 2 * pair + j, u:256:2]
+                        nc.tensor.transpose(bank[:, j, u, :], src, ident[:])
 
         def copy_x(h, kg, engine="S"):
             grouped = work.tile([P, 2048], BF16, name="x_grouped", align_bytes=64)
@@ -218,6 +254,22 @@ def tile_dequant_linear_shifted_relu_g4_kernel(
             nc.vector.quantize_mx(
                 out=x_codes[h, kg][:].bitcast(FP8X4), scales=x_planes[h, kg][:], in_=tiles["xg", h, kg][:]
             )
+
+        def warm_quant():
+            nc.vector.quantize_mx(out=warm_codes[:].bitcast(FP8X4), scales=warm_plane[:], in_=vec_rows[:])
+
+        def warm(count):
+            bank = psum.tile([P, P], F32, name=f"warm{len(tiles)}_{len(turns)}", tag="acc3")
+            for i in range(count):
+                nc.tensor.matmul_mx(
+                    out=bank[:],
+                    lhsT=w_raw[0][:, 0:256].bitcast(FP4X4),
+                    lhsT_scale=warm_plane[:],
+                    rhs=warm_codes[:].bitcast(FP8X4),
+                    rhs_scale=warm_plane[:],
+                    start=True,
+                    stop=True,
+                )
 
         def perm_s(g):
             src = ws_raw[:, :, 512 * g : 512 * (g + 1)].rearrange("p k (m t) -> p t k m", t=4)
@@ -309,22 +361,22 @@ def tile_dequant_linear_shifted_relu_g4_kernel(
                     )
 
         def copy_y(s, j, engine):
-            rows = work.tile([P, 512], F32, name="y_rows", bufs=12)
-            tiles["yo", s, j] = rows
+            if j % 2 == 0:
+                tiles["yo", s, j // 2] = work.tile([P, 2, 512], F32, name="y_rows", bufs=6)
             copy_on(
                 engine,
-                rows[:].rearrange("p (c t) -> p c t", t=4),
+                tiles["yo", s, j // 2][:, j % 2, :].rearrange("p (c t) -> p c t", t=4),
                 tiles["yt", s, j][:].rearrange("p t c -> p c t"),
             )
 
         def store_y(s, lo, hi):
             g, h = BLOCKS[s]
-            for j in range(lo, hi):
-                row0 = 512 * h + P * j
-                nc.sync.dma_start(out=out_0[row0 : row0 + P, 512 * g : 512 * (g + 1)], in_=tiles["yo", s, j][:])
+            rows = out_0[512 * h + P * lo : 512 * h + P * hi, 512 * g : 512 * (g + 1)]
+            src = tiles["yo", s, lo // 2][:, lo % 2 : lo % 2 + hi - lo, :]
+            nc.sync.dma_start(out=rows.rearrange("(j p) n -> p j n", p=P), in_=src)
 
         steps = dict(
-            setup=setup, load_vec=load_vec, load_x=load_x, load_ws=load_ws, load_w=load_w, spread_ts=spread_ts, turn_x=turn_x,
+            setup=setup, spread_vec=spread_vec, pair_x=pair_x, warm=warm, warm_quant=warm_quant, load_vec=load_vec, load_x=load_x, load_ws=load_ws, load_w=load_w, spread_ts=spread_ts, turn_x=turn_x,
             copy_x=copy_x, quant_x=quant_x, perm_s=perm_s, perm_c=perm_c, mx=mx, scale=scale, clamp=clamp,
             weave=weave, quant_y=quant_y, store_q=store_q, store_s=store_s, turn_y=turn_y, copy_y=copy_y,
             store_y=store_y,

@@ -17,11 +17,11 @@ ALU = mybir.AluOpType
 
 P = 128
 
-BLOCKS = [(0, 0), (1, 0), (0, 1), (1, 1), (2, 0), (2, 1), (3, 0), (3, 1)]
+BLOCKS = [(0, 0, 512), (1, 0, 512), (0, 512, 512), (1, 512, 512), (2, 0, 512), (2, 512, 512), (3, 0, 512), (3, 512, 512)]
 
 
-def schedule(vshare=(0, 0, 0, 0, 0, 128, 256), turn_after=(3, 2, 2, 2, 2, 2, 1), tmajor=(0, 0, 0, 0, 0, 0, 0),
-             wfirst=(1, 1, 1, 1, 1, 1, 1), qpos=(4, 2, 2, 2, 2, 2, 1), vpos=(0, 0, 0, 0, 0, 0, 0), last_v=512, last_eng="SSSS", reorder=0):
+def schedule(vshare=(0, 0, 0, 0, 0, 128, 256, 0), turn_after=(2,) * 8, tmajor=(0,) * 8, wfirst=(1,) * 8,
+             qpos=(4, 2, 2, 2, 2, 2, 2, 2), vpos=(0,) * 8, gshare=(0,) * 8, last_v=512, last_eng="SSSS", reorder=1):
     ops = []
     add = lambda *op: ops.append(op)
     add("setup")
@@ -37,8 +37,8 @@ def schedule(vshare=(0, 0, 0, 0, 0, 128, 256), turn_after=(3, 2, 2, 2, 2, 2, 1),
     add("copy_x", 0, 0)
     add("spread_vec")
     add("warm", 4)
-    add("quant_x", 0, 0)
     add("perm_s", 1)
+    add("quant_x", 0, 0)
     add("turn_x", 0, 1)
     add("copy_x", 0, 1)
     add("perm_s", 2)
@@ -49,28 +49,29 @@ def schedule(vshare=(0, 0, 0, 0, 0, 128, 256), turn_after=(3, 2, 2, 2, 2, 2, 1),
     add("copy_x", 0, 2)
     add("perm_c", 1, 0)
     add("perm_c", 1, 1)
+    add("perm_c", 1, 2)
     add("quant_x", 0, 2)
     for t in range(4):
         add("mx", 0, t, 1)
-    add("perm_c", 1, 2)
+    add("perm_c", 1, 3)
     if reorder:
         add("pair_x", 1, 0)
         add("pair_x", 1, 1)
     fills = {
-        0: [[("perm_c", 1, 3)], [], [("perm_s", 3)], []],
-        1: [[("quant_x", 1, 0)], [("quant_x", 1, 1)], [("quant_x", 1, 2)], []],
+        0: [[], [("perm_s", 3)], [], []],
+        1: [[], [("quant_x", 1, 0), ("quant_x", 1, 1)], [("quant_x", 1, 2)], []],
         2: [[], [("perm_c", 2, 0)], [("perm_c", 2, 1)], []],
-        3: [[("perm_c", 2, 2)], [("perm_c", 2, 3)], [], []],
-        4: [[("perm_c", 3, 0)], [("perm_c", 3, 1)], [], []],
-        5: [[("perm_c", 3, 2)], [("perm_c", 3, 3)], [], []],
-        6: [[], [], [], []], 7: [[], [], [], []]}
+        3: [[], [("perm_c", 2, 2)], [("perm_c", 2, 3)], []],
+        4: [[], [("perm_c", 3, 0)], [("perm_c", 3, 1)], []],
+        5: [[], [("perm_c", 3, 2)], [("perm_c", 3, 3)], []]}
     def quant_out(s):
         add("quant_y", s)
         add("store_q", s)
         if s == 5:
             add("store_s", 0, 3)
-    for s in range(8):
-        last = s == 7
+    final = len(BLOCKS) - 1
+    for s in range(final + 1):
+        last = s == final
         r = s - 1
         for t in range(4):
             for kg in range(3) if s else [2]:
@@ -79,32 +80,33 @@ def schedule(vshare=(0, 0, 0, 0, 0, 128, 256), turn_after=(3, 2, 2, 2, 2, 2, 1),
                 for kg in range(2):
                     add("turn_x", 1, kg)
                     add("copy_x", 1, kg)
-                if reorder:
+                if reorder == 2:
                     add("pair_x", 1, 2)
             if s == 1 and t == 1:
                 add("turn_x", 1, 2)
                 add("copy_x", 1, 2)
             if s >= 1:
-                if wfirst[r] and t == (1 if s == 1 else 0) and vshare[r] < 512:
-                    add("weave", r, vshare[r], 512, "S")
+                width = BLOCKS[r][2] - gshare[r]
+                js = range(4)
+                if wfirst[r] and t == (1 if s == 1 else 0) and vshare[r] < width:
+                    add("weave", r, vshare[r], width, "S")
                 if t == turn_after[r]:
                     if tmajor[r]:
                         for u in range(4):
-                            add("turn_y", r, range(4), [u])
+                            add("turn_y", r, js, [u])
                     else:
-                        add("turn_y", r, range(4), range(4))
-                    for j in range(4):
+                        add("turn_y", r, js, range(4))
+                    for j in js:
                         add("copy_y", r, j, "S")
-                        if j % 2:
-                            add("store_y", r, j - 1, j + 1)
-                    if not wfirst[r] and vshare[r] < 512:
-                        add("weave", r, vshare[r], 512, "S")
+                        add("store_y", r, j, j + 1)
+                    if not wfirst[r] and vshare[r] < width:
+                        add("weave", r, vshare[r], width, "S")
             add("scale", s, t)
             if t >= 1:
                 add("clamp", s, t - 1)
             if s >= 1 and t == vpos[r] and vshare[r]:
                 add("weave", r, 0, vshare[r], "V")
-            for op in fills[s][t]:
+            for op in fills.get(s, [[], [], [], []])[t]:
                 add(*op)
             if s >= 2 and qpos[s - 2] == 4 + t:
                 quant_out(s - 2)
@@ -112,22 +114,23 @@ def schedule(vshare=(0, 0, 0, 0, 0, 128, 256), turn_after=(3, 2, 2, 2, 2, 2, 1),
                 quant_out(r)
             if t == 3 and last:
                 for u in range(3):
-                    add("turn_y", s, range(4), [u])
+                    add("turn_y", s, range(BLOCKS[s][2] // 128), [u])
         add("clamp", s, 3)
-    add("turn_y", 7, range(4), [3])
-    if qpos[6] == 4:
-        quant_out(6)
-    add("weave", 7, 0, last_v, "V")
-    if last_v < 512:
-        add("weave", 7, last_v, 512, "S")
-    for j in range(3):
-        add("copy_y", 7, j, last_eng[j])
-        if j:
-            add("store_y", 7, 0 if j == 1 else j, j + 1)
-    add("quant_y", 7)
-    add("store_q", 7)
-    add("copy_y", 7, 3, last_eng[3])
-    add("store_y", 7, 3, 4)
+        if gshare[s] and not last:
+            add("weave", s, 512 - gshare[s], 512, "G")
+    js = range(BLOCKS[final][2] // 128)
+    add("turn_y", final, js, [3])
+    if qpos[final - 1] == 4:
+        quant_out(final - 1)
+    add("weave", final, 0, last_v, "V")
+    if last_v < BLOCKS[final][2]:
+        add("weave", final, last_v, BLOCKS[final][2], "S")
+    for j in js:
+        if j == len(js) - 1:
+            add("quant_y", final)
+            add("store_q", final)
+        add("copy_y", final, j, last_eng[j])
+        add("store_y", final, j, j + 1)
     add("store_s", 3, 4)
     return ops
 
@@ -281,7 +284,7 @@ def tile_dequant_linear_shifted_relu_g4_kernel(
             nc.vector.tensor_copy(out=dst, in_=src)
 
         def mx(s, t, kg):
-            g, h = BLOCKS[s]
+            g, h = BLOCKS[s][0], BLOCKS[s][1] // 512
             if kg == 0:
                 tiles["acc", s, t] = psum.tile([P, 512], F32, name=f"acc{s}{t}", tag=f"acc{t}")
             nc.tensor.matmul_mx(
@@ -295,7 +298,7 @@ def tile_dequant_linear_shifted_relu_g4_kernel(
             )
 
         def scale(s, t):
-            g, h = BLOCKS[s]
+            g, h = BLOCKS[s][0], BLOCKS[s][1] // 512
             scaled = work.tile([P, 512], F32, name="scaled", bufs=6)
             tiles["v", s, t] = scaled
             nc.vector.scalar_tensor_tensor(
@@ -308,7 +311,7 @@ def tile_dequant_linear_shifted_relu_g4_kernel(
             )
 
         def clamp(s, t):
-            g, h = BLOCKS[s]
+            g, h = BLOCKS[s][0], BLOCKS[s][1] // 512
             if t == 0:
                 tiles["y", s] = work.tile([P, 4, 512], F32, name="y_turned")
             nc.vector.tensor_scalar(
@@ -328,7 +331,7 @@ def tile_dequant_linear_shifted_relu_g4_kernel(
             copy_on(engine, dst, src)
 
         def quant_y(s):
-            g, h = BLOCKS[s]
+            g, h = BLOCKS[s][0], BLOCKS[s][1] // 512
             codes = work.tile([P, 512], U32, name="y_codes", align_bytes=64)
             tiles["yq", s] = codes
             nc.vector.quantize_mx(
@@ -338,7 +341,7 @@ def tile_dequant_linear_shifted_relu_g4_kernel(
             )
 
         def store_q(s):
-            g, h = BLOCKS[s]
+            g, h = BLOCKS[s][0], BLOCKS[s][1] // 512
             dst = out_1[g].rearrange("p m t -> p (m t)").bitcast(I32)[:, 512 * h : 512 * (h + 1)]
             nc.sync.dma_start(out=dst, in_=tiles["yq", s][:].bitcast(I32))
 
@@ -361,19 +364,19 @@ def tile_dequant_linear_shifted_relu_g4_kernel(
                     )
 
         def copy_y(s, j, engine):
-            if j % 2 == 0:
-                tiles["yo", s, j // 2] = work.tile([P, 2, 512], F32, name="y_rows", bufs=6)
+            rows = work.tile([P, 512], F32, name="y_rows", bufs=12)
+            tiles["yo", s, j] = rows
             copy_on(
                 engine,
-                tiles["yo", s, j // 2][:, j % 2, :].rearrange("p (c t) -> p c t", t=4),
+                rows[:].rearrange("p (c t) -> p c t", t=4),
                 tiles["yt", s, j][:].rearrange("p t c -> p c t"),
             )
 
         def store_y(s, lo, hi):
-            g, h = BLOCKS[s]
-            rows = out_0[512 * h + P * lo : 512 * h + P * hi, 512 * g : 512 * (g + 1)]
-            src = tiles["yo", s, lo // 2][:, lo % 2 : lo % 2 + hi - lo, :]
-            nc.sync.dma_start(out=rows.rearrange("(j p) n -> p j n", p=P), in_=src)
+            g, h = BLOCKS[s][0], BLOCKS[s][1] // 512
+            for j in range(lo, hi):
+                row0 = 512 * h + P * j
+                nc.sync.dma_start(out=out_0[row0 : row0 + P, 512 * g : 512 * (g + 1)], in_=tiles["yo", s, j][:])
 
         steps = dict(
             setup=setup, spread_vec=spread_vec, pair_x=pair_x, warm=warm, warm_quant=warm_quant, load_vec=load_vec, load_x=load_x, load_ws=load_ws, load_w=load_w, spread_ts=spread_ts, turn_x=turn_x,

@@ -16,123 +16,23 @@ FP4X4 = mybir.dt.float4_e2m1fn_x4
 ALU = mybir.AluOpType
 
 P = 128
+SLOTS = 4
+SPAN = P * SLOTS
+PASSES = K // SPAN
+GROUPS = N // SPAN
+HALVES = M // SPAN
+TILES = SPAN // P
+QUADRANTS = 4
+W_ROW_BYTES = 2 * SPAN
+PAIR_WORDS = SPAN // 2
+PLANE_ROWS = 112
+TURN_BANKS = 4
 
-BLOCKS = [(0, 0, 512), (1, 0, 512), (0, 512, 512), (1, 512, 512), (2, 0, 512), (2, 512, 512), (3, 0, 512), (3, 512, 512)]
+BLOCKS = [(0, 0), (1, 0), (0, 1), (1, 1), (2, 0), (2, 1), (3, 0), (3, 1)]
+LAST = len(BLOCKS) - 1
 
-
-def schedule(vshare=(0, 0, 0, 0, 0, 128, 256, 0), turn_after=(2,) * 8, tmajor=(0,) * 8, wfirst=(1,) * 8,
-             qpos=(4, 2, 2, 2, 2, 2, 2, 2), vpos=(0,) * 8, gshare=(0,) * 8, last_v=512, last_eng="SSSS", reorder=1):
-    ops = []
-    add = lambda *op: ops.append(op)
-    add("setup")
-    for op in [("load_vec",), ("load_w", 0), ("load_x", 0, 0), ("load_ws",), ("load_x", 0, 1), ("load_x", 0, 2), ("load_w", 1), ("load_x", 1, 0), ("load_x", 1, 1), ("load_x", 1, 2), ("load_w", 2), ("load_w", 3)]:
-        add(*op)
-    add("warm_quant")
-    add("spread_ts")
-    add("warm", 10)
-    for t in range(4):
-        add("perm_c", 0, t)
-    add("perm_s", 0)
-    add("turn_x", 0, 0)
-    add("copy_x", 0, 0)
-    add("spread_vec")
-    add("warm", 4)
-    add("perm_s", 1)
-    add("quant_x", 0, 0)
-    add("turn_x", 0, 1)
-    add("copy_x", 0, 1)
-    add("perm_s", 2)
-    add("quant_x", 0, 1)
-    for t in range(4):
-        add("mx", 0, t, 0)
-    add("turn_x", 0, 2)
-    add("copy_x", 0, 2)
-    add("perm_c", 1, 0)
-    add("perm_c", 1, 1)
-    add("perm_c", 1, 2)
-    add("quant_x", 0, 2)
-    for t in range(4):
-        add("mx", 0, t, 1)
-    add("perm_c", 1, 3)
-    if reorder:
-        add("pair_x", 1, 0)
-        add("pair_x", 1, 1)
-    fills = {
-        0: [[], [("perm_s", 3)], [], []],
-        1: [[], [("quant_x", 1, 0), ("quant_x", 1, 1)], [("quant_x", 1, 2)], []],
-        2: [[], [("perm_c", 2, 0)], [("perm_c", 2, 1)], []],
-        3: [[], [("perm_c", 2, 2)], [("perm_c", 2, 3)], []],
-        4: [[], [("perm_c", 3, 0)], [("perm_c", 3, 1)], []],
-        5: [[], [("perm_c", 3, 2)], [("perm_c", 3, 3)], []]}
-    def quant_out(s):
-        add("quant_y", s)
-        add("store_q", s)
-        if s == 5:
-            add("store_s", 0, 3)
-    final = len(BLOCKS) - 1
-    for s in range(final + 1):
-        last = s == final
-        r = s - 1
-        for t in range(4):
-            for kg in range(3) if s else [2]:
-                add("mx", s, t, kg)
-            if s == 0 and t == 3:
-                for kg in range(2):
-                    add("turn_x", 1, kg)
-                    add("copy_x", 1, kg)
-                if reorder == 2:
-                    add("pair_x", 1, 2)
-            if s == 1 and t == 1:
-                add("turn_x", 1, 2)
-                add("copy_x", 1, 2)
-            if s >= 1:
-                width = BLOCKS[r][2] - gshare[r]
-                js = range(4)
-                if wfirst[r] and t == (1 if s == 1 else 0) and vshare[r] < width:
-                    add("weave", r, vshare[r], width, "S")
-                if t == turn_after[r]:
-                    if tmajor[r]:
-                        for u in range(4):
-                            add("turn_y", r, js, [u])
-                    else:
-                        add("turn_y", r, js, range(4))
-                    for j in js:
-                        add("copy_y", r, j, "S")
-                        add("store_y", r, j, j + 1)
-                    if not wfirst[r] and vshare[r] < width:
-                        add("weave", r, vshare[r], width, "S")
-            add("scale", s, t)
-            if t >= 1:
-                add("clamp", s, t - 1)
-            if s >= 1 and t == vpos[r] and vshare[r]:
-                add("weave", r, 0, vshare[r], "V")
-            for op in fills.get(s, [[], [], [], []])[t]:
-                add(*op)
-            if s >= 2 and qpos[s - 2] == 4 + t:
-                quant_out(s - 2)
-            if s >= 1 and qpos[r] == t:
-                quant_out(r)
-            if t == 3 and last:
-                for u in range(3):
-                    add("turn_y", s, range(BLOCKS[s][2] // 128), [u])
-        add("clamp", s, 3)
-        if gshare[s] and not last:
-            add("weave", s, 512 - gshare[s], 512, "G")
-    js = range(BLOCKS[final][2] // 128)
-    add("turn_y", final, js, [3])
-    if qpos[final - 1] == 4:
-        quant_out(final - 1)
-    add("weave", final, 0, last_v, "V")
-    if last_v < BLOCKS[final][2]:
-        add("weave", final, last_v, BLOCKS[final][2], "S")
-    for j in js:
-        if j == len(js) - 1:
-            add("quant_y", final)
-            add("store_q", final)
-        add("copy_y", final, j, last_eng[j])
-        add("store_y", final, j, j + 1)
-    add("store_s", 3, 4)
-    return ops
+WARM_FIRST, WARM_SECOND = 10, 6
+LATE_VECTOR_TOKENS = 256
 
 
 def tile_dequant_linear_shifted_relu_g4_kernel(
@@ -147,126 +47,135 @@ def tile_dequant_linear_shifted_relu_g4_kernel(
 
         ident = keep.tile([P, P], F32, name="ident")
         ident_bf = keep.tile([P, P], BF16, name="ident_bf")
-        ts_col = keep.tile([P, 8], BF16, name="ts_col")
+        ts_col = keep.tile([P, M // P], BF16, name="ts_col")
         ts_all = keep.tile([P, M], BF16, name="ts_all")
-        vec_rows = keep.tile([P, 512], BF16, name="vec_rows", align_bytes=64)
+        vec_rows = keep.tile([P, SPAN], BF16, name="vec_rows", align_bytes=64)
         warm_codes = keep.tile([P, P], U32, name="warm_codes", align_bytes=64)
         warm_plane = keep.tile([P, P], U8, name="warm_plane", align_bytes=64)
-        vec_cols = keep.tile([P, 4, 12], F32, name="vec_cols")
-        ws_raw = keep.tile([P, 3, N], U8, name="ws_raw", align_bytes=64)
-        y_scales = keep.tile([P, 4, M], U8, name="y_scales", align_bytes=64)
-        w_raw = [keep.tile([P, 3 * 1024], U8, name=f"w_raw{g}", align_bytes=64) for g in range(4)]
-        w_codes = [keep.tile([P, 4, 3, 256], U8, name=f"w_codes{g}", align_bytes=64) for g in range(4)]
-        w_planes = [keep.tile([P, 4, 3, P], U8, name=f"w_planes{g}", align_bytes=64) for g in range(4)]
+        vec_cols = keep.tile([P, SLOTS, 3 * GROUPS], F32, name="vec_cols")
+        ws_raw = keep.tile([P, N], U8, name="ws_raw", align_bytes=64)
+        y_scales = keep.tile([P, GROUPS, M], U8, name="y_scales", align_bytes=64)
+        w_raw = [
+            keep.tile([P, PASSES * W_ROW_BYTES], U8, name=f"w_raw{g}", align_bytes=64) for g in range(GROUPS)
+        ]
+        w_codes = [
+            keep.tile([P, SLOTS, PASSES, 2 * P], U8, name=f"w_codes{g}", align_bytes=64) for g in range(GROUPS)
+        ]
+        w_planes = {}
+        for duo in range(GROUPS // 2):
+            for kp in range(PASSES):
+                w_planes[duo, kp] = keep.tile([P, 2, SLOTS, P], U8, name=f"w_planes{duo}{kp}", align_bytes=64)
         x_raw, x_codes, x_planes = {}, {}, {}
-        for h in range(2):
-            for kg in range(3):
-                x_raw[h, kg] = keep.tile([P, 4, 512], BF16, name=f"x_raw{h}{kg}", align_bytes=64)
-                x_codes[h, kg] = keep.tile([P, 512], U32, name=f"x_codes{h}{kg}", align_bytes=64)
-                x_planes[h, kg] = keep.tile([P, 512], U8, name=f"x_planes{h}{kg}", align_bytes=64)
+        for h in range(HALVES):
+            for kp in range(PASSES):
+                x_raw[h, kp] = keep.tile([P, TILES, SPAN], BF16, name=f"x_raw{h}{kp}", align_bytes=64)
+                x_codes[h, kp] = keep.tile([P, SPAN], U32, name=f"x_codes{h}{kp}", align_bytes=64)
+                x_planes[h, kp] = keep.tile([P, SPAN], U8, name=f"x_planes{h}{kp}", align_bytes=64)
 
-        tiles = {}
+        x_paired, x_grouped = {}, {}
+        acc, scaled, y_feat, y_grouped, y_banks = {}, {}, {}, {}, {}
         turns = []
 
         def turn_bank(shape, dtype):
-            tag = f"turn{len(turns) % 4}"
+            tag = f"turn{len(turns) % TURN_BANKS}"
             turns.append(tag)
             return psum.tile(shape, dtype, name=f"bank{len(turns)}", tag=tag)
 
-        def copy_on(engine, out, in_):
-            if engine == "S":
-                nc.scalar.copy(out=out, in_=in_)
-            else:
-                nc.vector.tensor_copy(out=out, in_=in_)
 
-        def setup():
-            nc.vector.memset(vec_rows[:], 0.0)
-            ws_words = ws_raw[:].rearrange("p k n -> p (k n)").bitcast(I32)
-            nc.vector.memset(ws_words, 0)
-            make_identity(nc, ident[:])
-            nc.vector.tensor_copy(out=ident_bf[:], in_=ident[:])
-
-        def load_vec():
-            nc.scalar.dma_start(out=ts_col[:], in_=token_scale.rearrange("(p j) -> p j", j=8))
-            for i, vec in enumerate((channel_scale, bias, floor_value)):
-                nc.scalar.dma_start(out=vec_rows[4 * i : 4 * i + 4, :], in_=vec.rearrange("(g c) -> g c", g=4))
-
-        def load_x(h, kg):
-            rows = x[512 * h : 512 * (h + 1), 512 * kg : 512 * (kg + 1)]
-            nc.sync.dma_start(out=x_raw[h, kg][:], in_=rows.rearrange("(j p) k -> p j k", p=P))
-
-        def load_ws():
-            src = w_scales.bitcast(I32)
-            dst = ws_raw[:].bitcast(I32)
-            for q in range(4):
-                nc.sync.dma_start(
-                    out=dst[32 * q : 32 * q + 4, :, :],
-                    in_=src[:, 4 * q : 4 * q + 4, :].rearrange("k r n -> r k n"),
-                )
+        def load_x(h, kp):
+            rows = x[SPAN * h : SPAN * (h + 1), SPAN * kp : SPAN * (kp + 1)]
+            nc.sync.dma_start(out=x_raw[h, kp][:], in_=rows.rearrange("(j p) k -> p j k", p=P))
 
         def load_w(g):
-            src = w_words.bitcast(I32)[:, :, 256 * g : 256 * (g + 1)]
-            dst = w_raw[g][:].bitcast(I32).rearrange("p (k n) -> p k n", k=3)
+            words = W_ROW_BYTES // 4
+            src = w_words.bitcast(I32)[:, :, words * g : words * (g + 1)]
+            dst = w_raw[g][:].bitcast(I32).rearrange("p (k n) -> p k n", k=PASSES)
             nc.sync.dma_start(out=dst, in_=src.rearrange("k p n -> p k n"))
 
-        def spread_ts():
-            bank = turn_bank([P, 8, P], BF16)
-            for j in range(8):
+        def load_w_scales():
+            src = w_scales.bitcast(I32)
+            dst = ws_raw[:].bitcast(I32)
+            for q in range(QUADRANTS):
+                queue = nc.scalar if q < QUADRANTS // 2 else nc.sync
+                queue.dma_start(out=dst[32 * q : 32 * q + 4 * PASSES, :], in_=src[:, 4 * q : 4 * q + 4, :])
+
+        def load_channel_vectors():
+            for i, vec in enumerate((channel_scale, bias, floor_value)):
+                rows = vec_rows[GROUPS * i : GROUPS * (i + 1), :]
+                nc.scalar.dma_start(out=rows, in_=vec.rearrange("(g c) -> g c", g=GROUPS))
+
+
+        def spread_token_scale():
+            per_row = M // P
+            bank = turn_bank([P, per_row, P], BF16)
+            for j in range(per_row):
                 nc.tensor.transpose(bank[:, j, :], ts_col[:, j : j + 1].to_broadcast([P, P]), ident_bf[:])
             nc.scalar.copy(
-                out=ts_all[:].rearrange("p (r j) -> p r j", j=8), in_=bank[:].rearrange("p j r -> p r j")
+                out=ts_all[:].rearrange("p (r j) -> p r j", j=per_row), in_=bank[:].rearrange("p j r -> p r j")
             )
 
-        def spread_vec():
-            bank = turn_bank([P, 4, P], BF16)
-            for t in range(4):
-                nc.tensor.transpose(bank[:, t, :], vec_rows[:, t:512:4], ident_bf[:])
-            nc.scalar.copy(out=vec_cols[:], in_=bank[:, :, 0:12])
+        def turn_channel_vectors():
+            bank = turn_bank([P, SLOTS, P], BF16)
+            for t in range(SLOTS):
+                nc.tensor.transpose(bank[:, t, :], vec_rows[:, t:SPAN:SLOTS], ident_bf[:])
+            nc.scalar.copy(out=vec_cols[:], in_=bank[:, :, 0 : 3 * GROUPS])
 
-        def pair_x(h, kg):
-            paired = work.tile([P, 4, 2, P], F32, name="x_paired", bufs=3)
-            tiles["xp", h, kg] = paired
-            words = x_raw[h, kg][:].bitcast(F32)
-            nc.scalar.copy(out=paired[:], in_=words.rearrange("p j (c u) -> p j u c", u=2))
+        def channel_col(i, g, t):
+            return vec_cols[:, t, GROUPS * i + g : GROUPS * i + g + 1]
 
-        def turn_x(h, kg):
-            words = x_raw[h, kg][:].bitcast(F32)
-            for pair in range(2):
-                bank = turn_bank([P, 2, 2, P], F32)
-                tiles["xt", h, kg, pair] = bank
+
+        def pair_x(h, kp):
+            x_paired[h, kp] = work.tile([P, TILES, 2, P], F32, name="x_paired", bufs=PASSES)
+            words = x_raw[h, kp][:].bitcast(F32)
+            nc.scalar.copy(out=x_paired[h, kp][:], in_=words.rearrange("p j (c u) -> p j u c", u=2))
+
+        def turn_x(h, kp):
+            words = x_raw[h, kp][:].bitcast(F32)
+            banks = []
+            for pair in range(TILES // 2):
+                banks.append(turn_bank([P, 2, 2, P], F32))
                 for j in range(2):
                     for u in range(2):
-                        if ("xp", h, kg) in tiles:
-                            src = tiles["xp", h, kg][:, 2 * pair + j, u, :]
+                        if (h, kp) in x_paired:
+                            src = x_paired[h, kp][:, 2 * pair + j, u, :]
                         else:
-                            src = words[:, 2 * pair + j, u:256:2]
-                        nc.tensor.transpose(bank[:, j, u, :], src, ident[:])
-
-        def copy_x(h, kg, engine="S"):
-            grouped = work.tile([P, 2048], BF16, name="x_grouped", align_bytes=64)
-            tiles["xg", h, kg] = grouped
-            words = grouped[:].bitcast(F32)
-            for pair in range(2):
-                copy_on(
-                    engine,
-                    words[:, 512 * pair : 512 * (pair + 1)].rearrange("p (j r u) -> p j r u", j=2, u=2),
-                    tiles["xt", h, kg, pair][:].rearrange("p j u r -> p j r u"),
+                            src = words[:, 2 * pair + j, u:PAIR_WORDS:2]
+                        nc.tensor.transpose(banks[pair][:, j, u, :], src, ident[:])
+            x_grouped[h, kp] = work.tile([P, SPAN * SLOTS], BF16, name="x_grouped", align_bytes=64)
+            grouped = x_grouped[h, kp][:].bitcast(F32)
+            for pair in range(TILES // 2):
+                nc.scalar.copy(
+                    out=grouped[:, SPAN * pair : SPAN * (pair + 1)].rearrange("p (j r u) -> p j r u", j=2, u=2),
+                    in_=banks[pair][:].rearrange("p j u r -> p j r u"),
                 )
 
-        def quant_x(h, kg):
+        def quantize_x(h, kp):
             nc.vector.quantize_mx(
-                out=x_codes[h, kg][:].bitcast(FP8X4), scales=x_planes[h, kg][:], in_=tiles["xg", h, kg][:]
+                out=x_codes[h, kp][:].bitcast(FP8X4), scales=x_planes[h, kp][:], in_=x_grouped[h, kp][:]
             )
 
-        def warm_quant():
-            nc.vector.quantize_mx(out=warm_codes[:].bitcast(FP8X4), scales=warm_plane[:], in_=vec_rows[:])
 
-        def warm(count):
-            bank = psum.tile([P, P], F32, name=f"warm{len(tiles)}_{len(turns)}", tag="acc3")
+        def order_w_words(g, first_slot, count):
+            some = slice(first_slot, first_slot + count)
+            src = w_raw[g][:].rearrange("p (c t b) -> p t c b", t=SLOTS, b=2)[:, some, :, :]
+            dst = w_codes[g][:, some, :, :].rearrange("p t k (m b) -> p t (k m) b", b=2)
+            nc.vector.tensor_copy(out=dst, in_=src)
+
+        def order_w_scales(duo):
+            cols = ws_raw[:, 2 * SPAN * duo : 2 * SPAN * (duo + 1)]
+            nc.vector.tensor_copy(out=w_planes[duo, 0][:], in_=cols.rearrange("p (g m t) -> p g t m", g=2, t=SLOTS))
+            src = w_planes[duo, 0][:].rearrange("p g t m -> p (g t m)").bitcast(I32)
+            for kp in range(1, PASSES):
+                dst = w_planes[duo, kp][:].rearrange("p g t m -> p (g t m)").bitcast(I32)
+                nc.sync.dma_start(out=dst[0:PLANE_ROWS, :], in_=src[4 * kp : 4 * kp + PLANE_ROWS, :])
+
+
+        def warm_up(count):
+            bank = psum.tile([P, P], F32, name=f"warm{count}", tag=f"acc{SLOTS - 1}")
             for i in range(count):
                 nc.tensor.matmul_mx(
                     out=bank[:],
-                    lhsT=w_raw[0][:, 0:256].bitcast(FP4X4),
+                    lhsT=w_raw[0][:, 0 : 2 * P].bitcast(FP4X4),
                     lhsT_scale=warm_plane[:],
                     rhs=warm_codes[:].bitcast(FP8X4),
                     rhs_scale=warm_plane[:],
@@ -274,115 +183,176 @@ def tile_dequant_linear_shifted_relu_g4_kernel(
                     stop=True,
                 )
 
-        def perm_s(g):
-            src = ws_raw[:, :, 512 * g : 512 * (g + 1)].rearrange("p k (m t) -> p t k m", t=4)
-            nc.vector.tensor_copy(out=w_planes[g][:], in_=src)
-
-        def perm_c(g, t):
-            src = w_raw[g][:].rearrange("p (c t b) -> p t c b", t=4, b=2)[:, t, :, :]
-            dst = w_codes[g][:, t, :, :].rearrange("p k (m b) -> p (k m) b", b=2)
-            nc.vector.tensor_copy(out=dst, in_=src)
-
-        def mx(s, t, kg):
-            g, h = BLOCKS[s][0], BLOCKS[s][1] // 512
-            if kg == 0:
-                tiles["acc", s, t] = psum.tile([P, 512], F32, name=f"acc{s}{t}", tag=f"acc{t}")
+        def multiply(s, t, kp):
+            g, h = BLOCKS[s]
+            if kp == 0:
+                acc[s, t] = psum.tile([P, SPAN], F32, name=f"acc{s}{t}", tag=f"acc{t}")
             nc.tensor.matmul_mx(
-                out=tiles["acc", s, t][:],
-                lhsT=w_codes[g][:, t, kg, :].bitcast(FP4X4),
-                lhsT_scale=w_planes[g][:, t, kg, :],
-                rhs=x_codes[h, kg][:].bitcast(FP8X4),
-                rhs_scale=x_planes[h, kg][:],
-                start=(kg == 0),
-                stop=(kg == 2),
+                out=acc[s, t][:],
+                lhsT=w_codes[g][:, t, kp, :].bitcast(FP4X4),
+                lhsT_scale=w_planes[g // 2, kp][:, g % 2, t, :],
+                rhs=x_codes[h, kp][:].bitcast(FP8X4),
+                rhs_scale=x_planes[h, kp][:],
+                start=(kp == 0),
+                stop=(kp == PASSES - 1),
             )
 
         def scale(s, t):
-            g, h = BLOCKS[s][0], BLOCKS[s][1] // 512
-            scaled = work.tile([P, 512], F32, name="scaled", bufs=6)
-            tiles["v", s, t] = scaled
+            g, h = BLOCKS[s]
+            scaled[s, t] = work.tile([P, SPAN], F32, name="scaled", bufs=6)
             nc.vector.scalar_tensor_tensor(
-                out=scaled[:],
-                in0=tiles["acc", s, t][:],
-                scalar=vec_cols[:, t, g : g + 1],
-                in1=ts_all[:, 512 * h : 512 * (h + 1)],
+                out=scaled[s, t][:],
+                in0=acc[s, t][:],
+                scalar=channel_col(0, g, t),
+                in1=ts_all[:, SPAN * h : SPAN * (h + 1)],
                 op0=ALU.mult,
                 op1=ALU.mult,
             )
 
         def clamp(s, t):
-            g, h = BLOCKS[s][0], BLOCKS[s][1] // 512
+            g, h = BLOCKS[s]
             if t == 0:
-                tiles["y", s] = work.tile([P, 4, 512], F32, name="y_turned")
+                y_feat[s] = work.tile([P, SLOTS, SPAN], F32, name="y_turned")
             nc.vector.tensor_scalar(
-                out=tiles["y", s][:, t, :],
-                in0=tiles["v", s, t][:],
-                scalar1=vec_cols[:, t, 4 + g : 5 + g],
-                scalar2=vec_cols[:, t, 8 + g : 9 + g],
+                out=y_feat[s][:, t, :],
+                in0=scaled[s, t][:],
+                scalar1=channel_col(1, g, t),
+                scalar2=channel_col(2, g, t),
                 op0=ALU.add,
                 op1=ALU.max,
             )
 
-        def weave(s, lo, hi, engine):
-            if ("yb", s) not in tiles:
-                tiles["yb", s] = work.tile([P, 2048], BF16, name="y_grouped", align_bytes=64)
-            dst = tiles["yb", s][:, 4 * lo : 4 * hi].rearrange("p (c i t) -> p c t i", i=4, t=4)
-            src = tiles["y", s][:, :, lo:hi].rearrange("p t (c i) -> p c t i", i=4)
-            copy_on(engine, dst, src)
 
-        def quant_y(s):
-            g, h = BLOCKS[s][0], BLOCKS[s][1] // 512
-            codes = work.tile([P, 512], U32, name="y_codes", align_bytes=64)
-            tiles["yq", s] = codes
-            nc.vector.quantize_mx(
-                out=codes[:].bitcast(FP8X4),
-                scales=y_scales[:, g, 512 * h : 512 * (h + 1)],
-                in_=tiles["yb", s][:],
-            )
+        def group_y(s, lo, hi, copy):
+            if s not in y_grouped:
+                y_grouped[s] = work.tile([P, SPAN * SLOTS], BF16, name="y_grouped", align_bytes=64)
+            dst = y_grouped[s][:, SLOTS * lo : SLOTS * hi].rearrange("p (c i t) -> p c t i", i=4, t=SLOTS)
+            src = y_feat[s][:, :, lo:hi].rearrange("p t (c i) -> p c t i", i=4)
+            copy(out=dst, in_=src)
 
-        def store_q(s):
-            g, h = BLOCKS[s][0], BLOCKS[s][1] // 512
-            dst = out_1[g].rearrange("p m t -> p (m t)").bitcast(I32)[:, 512 * h : 512 * (h + 1)]
-            nc.sync.dma_start(out=dst, in_=tiles["yq", s][:].bitcast(I32))
+        def quantize_y(s):
+            g, h = BLOCKS[s]
+            tokens = slice(SPAN * h, SPAN * (h + 1))
+            codes = work.tile([P, SPAN], U32, name="y_codes", align_bytes=64)
+            nc.vector.quantize_mx(out=codes[:].bitcast(FP8X4), scales=y_scales[:, g, tokens], in_=y_grouped[s][:])
+            dst = out_1[g].rearrange("p m t -> p (m t)").bitcast(I32)[:, tokens]
+            nc.sync.dma_start(out=dst, in_=codes[:].bitcast(I32))
 
-        def store_s(lo, hi):
+        def store_y_scales(lo, hi):
             dst = out_2.bitcast(I32)
             src = y_scales[:].bitcast(I32)
-            for q in range(4):
+            for q in range(QUADRANTS):
                 nc.sync.dma_start(
                     out=dst[lo:hi, 4 * q : 4 * q + 4, :].rearrange("g r m -> r g m"),
                     in_=src[32 * q : 32 * q + 4, lo:hi, :],
                 )
 
-        def turn_y(s, js, ts):
-            for j in js:
-                if ("yt", s, j) not in tiles:
-                    tiles["yt", s, j] = turn_bank([P, 4, P], F32)
-                for t in ts:
-                    nc.tensor.transpose(
-                        tiles["yt", s, j][:, t, :], tiles["y", s][:, t, P * j : P * (j + 1)], ident[:]
-                    )
 
-        def copy_y(s, j, engine):
-            rows = work.tile([P, 512], F32, name="y_rows", bufs=12)
-            tiles["yo", s, j] = rows
-            copy_on(
-                engine,
-                rows[:].rearrange("p (c t) -> p c t", t=4),
-                tiles["yt", s, j][:].rearrange("p t c -> p c t"),
+        def turn_y(s, j, t):
+            if t == 0:
+                y_banks[s, j] = turn_bank([P, SLOTS, P], F32)
+            nc.tensor.transpose(y_banks[s, j][:, t, :], y_feat[s][:, t, P * j : P * (j + 1)], ident[:])
+
+        def store_y(s, j):
+            g, h = BLOCKS[s]
+            rows = work.tile([P, SPAN], F32, name="y_rows", bufs=12)
+            nc.scalar.copy(
+                out=rows[:].rearrange("p (c t) -> p c t", t=SLOTS), in_=y_banks[s, j][:].rearrange("p t c -> p c t")
             )
+            row0 = SPAN * h + P * j
+            nc.sync.dma_start(out=out_0[row0 : row0 + P, SPAN * g : SPAN * (g + 1)], in_=rows[:])
 
-        def store_y(s, lo, hi):
-            g, h = BLOCKS[s][0], BLOCKS[s][1] // 512
-            for j in range(lo, hi):
-                row0 = 512 * h + P * j
-                nc.sync.dma_start(out=out_0[row0 : row0 + P, 512 * g : 512 * (g + 1)], in_=tiles["yo", s, j][:])
 
-        steps = dict(
-            setup=setup, spread_vec=spread_vec, pair_x=pair_x, warm=warm, warm_quant=warm_quant, load_vec=load_vec, load_x=load_x, load_ws=load_ws, load_w=load_w, spread_ts=spread_ts, turn_x=turn_x,
-            copy_x=copy_x, quant_x=quant_x, perm_s=perm_s, perm_c=perm_c, mx=mx, scale=scale, clamp=clamp,
-            weave=weave, quant_y=quant_y, store_q=store_q, store_s=store_s, turn_y=turn_y, copy_y=copy_y,
-            store_y=store_y,
-        )
-        for op in schedule():
-            steps[op[0]](*op[1:])
+        nc.vector.memset(vec_rows[:], 0.0)
+        nc.vector.memset(ws_raw[:].bitcast(I32), 0)
+        make_identity(nc, ident[:])
+        for duo in range(GROUPS // 2):
+            for kp in range(1, PASSES):
+                nc.gpsimd.memset(w_planes[duo, kp][:].bitcast(I32), 0)
+        nc.vector.tensor_copy(out=ident_bf[:], in_=ident[:])
+        nc.vector.quantize_mx(out=warm_codes[:].bitcast(FP8X4), scales=warm_plane[:], in_=vec_rows[:])
+
+        nc.scalar.dma_start(out=ts_col[:], in_=token_scale.rearrange("(p j) -> p j", j=M // P))
+        load_w(0)
+        load_x(0, 0)
+        load_w_scales()
+        load_x(0, 1)
+        load_x(0, 2)
+        load_w(1)
+        spread_token_scale()
+        load_channel_vectors()
+        warm_up(WARM_FIRST)
+        order_w_words(0, 0, SLOTS)
+        order_w_scales(0)
+        for kp in range(PASSES):
+            load_x(1, kp)
+        turn_x(0, 0)
+        warm_up(WARM_SECOND)
+        order_w_scales(1)
+        load_w(2)
+        load_w(3)
+        quantize_x(0, 0)
+        turn_x(0, 1)
+        quantize_x(0, 1)
+        for t in range(SLOTS):
+            multiply(0, t, 0)
+        turn_x(0, 2)
+        turn_channel_vectors()
+        order_w_words(1, 0, SLOTS)
+        quantize_x(0, 2)
+        for t in range(SLOTS):
+            multiply(0, t, 1)
+        pair_x(1, 0)
+        pair_x(1, 1)
+
+        for s in range(LAST + 1):
+            vector_tokens = LATE_VECTOR_TOKENS if s == LAST else 0
+            group_slot, turn_slot = (1, 3) if s == 1 else (0, 2)
+            for t in range(SLOTS):
+                for kp in range(PASSES) if s else [PASSES - 1]:
+                    multiply(s, t, kp)
+                if (s, t) == (0, SLOTS - 1):
+                    turn_x(1, 0)
+                    turn_x(1, 1)
+                if (s, t) == (1, 1):
+                    turn_x(1, 2)
+                if s >= 1 and t == group_slot:
+                    group_y(s - 1, vector_tokens, SPAN, nc.scalar.copy)
+                if s >= 1 and t == turn_slot:
+                    for j in range(TILES):
+                        for slot in range(SLOTS):
+                            turn_y(s - 1, j, slot)
+                    for j in range(TILES):
+                        store_y(s - 1, j)
+
+                scale(s, t)
+                if t >= 1:
+                    clamp(s, t - 1)
+                if t == 1 and vector_tokens:
+                    group_y(s - 1, 0, vector_tokens, nc.vector.tensor_copy)
+                if (s, t) == (1, 1):
+                    quantize_x(1, 0)
+                    quantize_x(1, 1)
+                if (s, t) == (1, 2):
+                    quantize_x(1, 2)
+                if t == 1 and 2 <= s <= 5:
+                    order_w_words(s // 2 + 1, 2 * (s % 2), 2)
+                if t == 0 and s >= 2:
+                    quantize_y(s - 2)
+                    if s == LAST:
+                        store_y_scales(0, GROUPS - 1)
+            if s == LAST:
+                for slot in range(SLOTS - 1):
+                    for j in range(TILES):
+                        turn_y(s, j, slot)
+            clamp(s, SLOTS - 1)
+
+        for j in range(TILES):
+            turn_y(LAST, j, SLOTS - 1)
+        quantize_y(LAST - 1)
+        group_y(LAST, 0, SPAN, nc.vector.tensor_copy)
+        for j in range(TILES - 1):
+            store_y(LAST, j)
+        quantize_y(LAST)
+        store_y(LAST, TILES - 1)
+        store_y_scales(GROUPS - 1, GROUPS)

from contextlib import ExitStack

import concourse.mybir as mybir
from concourse.masks import make_identity

M, K, N = 1024, 1536, 2048
FLOPS = 2 * M * K * N

F32 = mybir.dt.float32
BF16 = mybir.dt.bfloat16
I32 = mybir.dt.int32
U32 = mybir.dt.uint32
U8 = mybir.dt.uint8
FP8X4 = mybir.dt.float8_e4m3fn_x4
FP4X4 = mybir.dt.float4_e2m1fn_x4
ALU = mybir.AluOpType

P = 128
SLOTS = 4
SPAN = P * SLOTS
PASSES = K // SPAN
GROUPS = N // SPAN
HALVES = M // SPAN
TILES = SPAN // P
QUADRANTS = 4
W_ROW_BYTES = 2 * SPAN
PAIR_WORDS = SPAN // 2
PLANE_ROWS = 112
TURN_BANKS = 4

BLOCKS = [(0, 0), (1, 0), (0, 1), (1, 1), (2, 0), (2, 1), (3, 0), (3, 1)]
LAST = len(BLOCKS) - 1

WARM_FIRST, WARM_SECOND = 10, 6
LATE_VECTOR_TOKENS = 256


def tile_dequant_linear_shifted_relu_g4_kernel(
    tc, x, w_words, w_scales, token_scale, channel_scale, bias, floor_value, out_0, out_1, out_2
):
    nc = tc.nc
    with ExitStack() as ctx:
        keep = ctx.enter_context(tc.tile_pool(name="keep", bufs=1))
        work = ctx.enter_context(tc.tile_pool(name="work", bufs=4))
        psum = ctx.enter_context(tc.psum_pool(name="psum", bufs=1))
        ctx.enter_context(tc.manual_schedule())

        ident = keep.tile([P, P], F32, name="ident")
        ident_bf = keep.tile([P, P], BF16, name="ident_bf")
        ts_col = keep.tile([P, M // P], BF16, name="ts_col")
        ts_all = keep.tile([P, M], BF16, name="ts_all")
        vec_rows = keep.tile([P, SPAN], BF16, name="vec_rows", align_bytes=64)
        warm_codes = keep.tile([P, P], U32, name="warm_codes", align_bytes=64)
        warm_plane = keep.tile([P, P], U8, name="warm_plane", align_bytes=64)
        vec_cols = keep.tile([P, SLOTS, 3 * GROUPS], F32, name="vec_cols")
        ws_raw = keep.tile([P, N], U8, name="ws_raw", align_bytes=64)
        y_scales = keep.tile([P, GROUPS, M], U8, name="y_scales", align_bytes=64)
        w_raw = [
            keep.tile([P, PASSES * W_ROW_BYTES], U8, name=f"w_raw{g}", align_bytes=64) for g in range(GROUPS)
        ]
        w_codes = [
            keep.tile([P, SLOTS, PASSES, 2 * P], U8, name=f"w_codes{g}", align_bytes=64) for g in range(GROUPS)
        ]
        w_planes = {}
        for duo in range(GROUPS // 2):
            for kp in range(PASSES):
                w_planes[duo, kp] = keep.tile([P, 2, SLOTS, P], U8, name=f"w_planes{duo}{kp}", align_bytes=64)
        x_raw, x_codes, x_planes = {}, {}, {}
        for h in range(HALVES):
            for kp in range(PASSES):
                x_raw[h, kp] = keep.tile([P, TILES, SPAN], BF16, name=f"x_raw{h}{kp}", align_bytes=64)
                x_codes[h, kp] = keep.tile([P, SPAN], U32, name=f"x_codes{h}{kp}", align_bytes=64)
                x_planes[h, kp] = keep.tile([P, SPAN], U8, name=f"x_planes{h}{kp}", align_bytes=64)

        x_paired, x_grouped = {}, {}
        acc, scaled, y_feat, y_grouped, y_banks = {}, {}, {}, {}, {}
        turns = []

        def turn_bank(shape, dtype):
            tag = f"turn{len(turns) % TURN_BANKS}"
            turns.append(tag)
            return psum.tile(shape, dtype, name=f"bank{len(turns)}", tag=tag)


        def load_x(h, kp):
            rows = x[SPAN * h : SPAN * (h + 1), SPAN * kp : SPAN * (kp + 1)]
            nc.sync.dma_start(out=x_raw[h, kp][:], in_=rows.rearrange("(j p) k -> p j k", p=P))

        def load_w(g):
            words = W_ROW_BYTES // 4
            src = w_words.bitcast(I32)[:, :, words * g : words * (g + 1)]
            dst = w_raw[g][:].bitcast(I32).rearrange("p (k n) -> p k n", k=PASSES)
            nc.sync.dma_start(out=dst, in_=src.rearrange("k p n -> p k n"))

        def load_w_scales():
            src = w_scales.bitcast(I32)
            dst = ws_raw[:].bitcast(I32)
            for q in range(QUADRANTS):
                queue = nc.scalar if q < QUADRANTS // 2 else nc.sync
                queue.dma_start(out=dst[32 * q : 32 * q + 4 * PASSES, :], in_=src[:, 4 * q : 4 * q + 4, :])

        def load_channel_vectors():
            for i, vec in enumerate((channel_scale, bias, floor_value)):
                rows = vec_rows[GROUPS * i : GROUPS * (i + 1), :]
                nc.scalar.dma_start(out=rows, in_=vec.rearrange("(g c) -> g c", g=GROUPS))


        def spread_token_scale():
            per_row = M // P
            bank = turn_bank([P, per_row, P], BF16)
            for j in range(per_row):
                nc.tensor.transpose(bank[:, j, :], ts_col[:, j : j + 1].to_broadcast([P, P]), ident_bf[:])
            nc.scalar.copy(
                out=ts_all[:].rearrange("p (r j) -> p r j", j=per_row), in_=bank[:].rearrange("p j r -> p r j")
            )

        def turn_channel_vectors():
            bank = turn_bank([P, SLOTS, P], BF16)
            for t in range(SLOTS):
                nc.tensor.transpose(bank[:, t, :], vec_rows[:, t:SPAN:SLOTS], ident_bf[:])
            nc.scalar.copy(out=vec_cols[:], in_=bank[:, :, 0 : 3 * GROUPS])

        def channel_col(i, g, t):
            return vec_cols[:, t, GROUPS * i + g : GROUPS * i + g + 1]


        def pair_x(h, kp):
            x_paired[h, kp] = work.tile([P, TILES, 2, P], F32, name="x_paired", bufs=PASSES)
            words = x_raw[h, kp][:].bitcast(F32)
            nc.scalar.copy(out=x_paired[h, kp][:], in_=words.rearrange("p j (c u) -> p j u c", u=2))

        def turn_x(h, kp):
            words = x_raw[h, kp][:].bitcast(F32)
            banks = []
            for pair in range(TILES // 2):
                banks.append(turn_bank([P, 2, 2, P], F32))
                for j in range(2):
                    for u in range(2):
                        if (h, kp) in x_paired:
                            src = x_paired[h, kp][:, 2 * pair + j, u, :]
                        else:
                            src = words[:, 2 * pair + j, u:PAIR_WORDS:2]
                        nc.tensor.transpose(banks[pair][:, j, u, :], src, ident[:])
            x_grouped[h, kp] = work.tile([P, SPAN * SLOTS], BF16, name="x_grouped", align_bytes=64)
            grouped = x_grouped[h, kp][:].bitcast(F32)
            for pair in range(TILES // 2):
                nc.scalar.copy(
                    out=grouped[:, SPAN * pair : SPAN * (pair + 1)].rearrange("p (j r u) -> p j r u", j=2, u=2),
                    in_=banks[pair][:].rearrange("p j u r -> p j r u"),
                )

        def quantize_x(h, kp):
            nc.vector.quantize_mx(
                out=x_codes[h, kp][:].bitcast(FP8X4), scales=x_planes[h, kp][:], in_=x_grouped[h, kp][:]
            )


        def order_w_words(g, first_slot, count):
            some = slice(first_slot, first_slot + count)
            src = w_raw[g][:].rearrange("p (c t b) -> p t c b", t=SLOTS, b=2)[:, some, :, :]
            dst = w_codes[g][:, some, :, :].rearrange("p t k (m b) -> p t (k m) b", b=2)
            nc.vector.tensor_copy(out=dst, in_=src)

        def order_w_scales(duo):
            cols = ws_raw[:, 2 * SPAN * duo : 2 * SPAN * (duo + 1)]
            nc.vector.tensor_copy(out=w_planes[duo, 0][:], in_=cols.rearrange("p (g m t) -> p g t m", g=2, t=SLOTS))
            src = w_planes[duo, 0][:].rearrange("p g t m -> p (g t m)").bitcast(I32)
            for kp in range(1, PASSES):
                dst = w_planes[duo, kp][:].rearrange("p g t m -> p (g t m)").bitcast(I32)
                nc.sync.dma_start(out=dst[0:PLANE_ROWS, :], in_=src[4 * kp : 4 * kp + PLANE_ROWS, :])


        def warm_up(count):
            bank = psum.tile([P, P], F32, name=f"warm{count}", tag=f"acc{SLOTS - 1}")
            for i in range(count):
                nc.tensor.matmul_mx(
                    out=bank[:],
                    lhsT=w_raw[0][:, 0 : 2 * P].bitcast(FP4X4),
                    lhsT_scale=warm_plane[:],
                    rhs=warm_codes[:].bitcast(FP8X4),
                    rhs_scale=warm_plane[:],
                    start=True,
                    stop=True,
                )

        def multiply(s, t, kp):
            g, h = BLOCKS[s]
            if kp == 0:
                acc[s, t] = psum.tile([P, SPAN], F32, name=f"acc{s}{t}", tag=f"acc{t}")
            nc.tensor.matmul_mx(
                out=acc[s, t][:],
                lhsT=w_codes[g][:, t, kp, :].bitcast(FP4X4),
                lhsT_scale=w_planes[g // 2, kp][:, g % 2, t, :],
                rhs=x_codes[h, kp][:].bitcast(FP8X4),
                rhs_scale=x_planes[h, kp][:],
                start=(kp == 0),
                stop=(kp == PASSES - 1),
            )

        def scale(s, t):
            g, h = BLOCKS[s]
            scaled[s, t] = work.tile([P, SPAN], F32, name="scaled", bufs=6)
            nc.vector.scalar_tensor_tensor(
                out=scaled[s, t][:],
                in0=acc[s, t][:],
                scalar=channel_col(0, g, t),
                in1=ts_all[:, SPAN * h : SPAN * (h + 1)],
                op0=ALU.mult,
                op1=ALU.mult,
            )

        def clamp(s, t):
            g, h = BLOCKS[s]
            if t == 0:
                y_feat[s] = work.tile([P, SLOTS, SPAN], F32, name="y_turned")
            nc.vector.tensor_scalar(
                out=y_feat[s][:, t, :],
                in0=scaled[s, t][:],
                scalar1=channel_col(1, g, t),
                scalar2=channel_col(2, g, t),
                op0=ALU.add,
                op1=ALU.max,
            )


        def group_y(s, lo, hi, copy):
            if s not in y_grouped:
                y_grouped[s] = work.tile([P, SPAN * SLOTS], BF16, name="y_grouped", align_bytes=64)
            dst = y_grouped[s][:, SLOTS * lo : SLOTS * hi].rearrange("p (c i t) -> p c t i", i=4, t=SLOTS)
            src = y_feat[s][:, :, lo:hi].rearrange("p t (c i) -> p c t i", i=4)
            copy(out=dst, in_=src)

        def quantize_y(s):
            g, h = BLOCKS[s]
            tokens = slice(SPAN * h, SPAN * (h + 1))
            codes = work.tile([P, SPAN], U32, name="y_codes", align_bytes=64)
            nc.vector.quantize_mx(out=codes[:].bitcast(FP8X4), scales=y_scales[:, g, tokens], in_=y_grouped[s][:])
            dst = out_1[g].rearrange("p m t -> p (m t)").bitcast(I32)[:, tokens]
            nc.sync.dma_start(out=dst, in_=codes[:].bitcast(I32))

        def store_y_scales(lo, hi):
            dst = out_2.bitcast(I32)
            src = y_scales[:].bitcast(I32)
            for q in range(QUADRANTS):
                nc.sync.dma_start(
                    out=dst[lo:hi, 4 * q : 4 * q + 4, :].rearrange("g r m -> r g m"),
                    in_=src[32 * q : 32 * q + 4, lo:hi, :],
                )


        def turn_y(s, j, t):
            if t == 0:
                y_banks[s, j] = turn_bank([P, SLOTS, P], F32)
            nc.tensor.transpose(y_banks[s, j][:, t, :], y_feat[s][:, t, P * j : P * (j + 1)], ident[:])

        def store_y(s, j):
            g, h = BLOCKS[s]
            rows = work.tile([P, SPAN], F32, name="y_rows", bufs=12)
            nc.scalar.copy(
                out=rows[:].rearrange("p (c t) -> p c t", t=SLOTS), in_=y_banks[s, j][:].rearrange("p t c -> p c t")
            )
            row0 = SPAN * h + P * j
            nc.sync.dma_start(out=out_0[row0 : row0 + P, SPAN * g : SPAN * (g + 1)], in_=rows[:])


        nc.vector.memset(vec_rows[:], 0.0)
        nc.vector.memset(ws_raw[:].bitcast(I32), 0)
        make_identity(nc, ident[:])
        for duo in range(GROUPS // 2):
            for kp in range(1, PASSES):
                nc.gpsimd.memset(w_planes[duo, kp][:].bitcast(I32), 0)
        nc.vector.tensor_copy(out=ident_bf[:], in_=ident[:])
        nc.vector.quantize_mx(out=warm_codes[:].bitcast(FP8X4), scales=warm_plane[:], in_=vec_rows[:])

        nc.scalar.dma_start(out=ts_col[:], in_=token_scale.rearrange("(p j) -> p j", j=M // P))
        load_w(0)
        load_x(0, 0)
        load_w_scales()
        load_x(0, 1)
        load_x(0, 2)
        load_w(1)
        spread_token_scale()
        load_channel_vectors()
        warm_up(WARM_FIRST)
        order_w_words(0, 0, SLOTS)
        order_w_scales(0)
        for kp in range(PASSES):
            load_x(1, kp)
        turn_x(0, 0)
        warm_up(WARM_SECOND)
        order_w_scales(1)
        load_w(2)
        load_w(3)
        quantize_x(0, 0)
        turn_x(0, 1)
        quantize_x(0, 1)
        for t in range(SLOTS):
            multiply(0, t, 0)
        turn_x(0, 2)
        turn_channel_vectors()
        order_w_words(1, 0, SLOTS)
        quantize_x(0, 2)
        for t in range(SLOTS):
            multiply(0, t, 1)
        pair_x(1, 0)
        pair_x(1, 1)

        for s in range(LAST + 1):
            vector_tokens = LATE_VECTOR_TOKENS if s == LAST else 0
            group_slot, turn_slot = (1, 3) if s == 1 else (0, 2)
            for t in range(SLOTS):
                for kp in range(PASSES) if s else [PASSES - 1]:
                    multiply(s, t, kp)
                if (s, t) == (0, SLOTS - 1):
                    turn_x(1, 0)
                    turn_x(1, 1)
                if (s, t) == (1, 1):
                    turn_x(1, 2)
                if s >= 1 and t == group_slot:
                    group_y(s - 1, vector_tokens, SPAN, nc.scalar.copy)
                if s >= 1 and t == turn_slot:
                    for j in range(TILES):
                        for slot in range(SLOTS):
                            turn_y(s - 1, j, slot)
                    for j in range(TILES):
                        store_y(s - 1, j)

                scale(s, t)
                if t >= 1:
                    clamp(s, t - 1)
                if t == 1 and vector_tokens:
                    group_y(s - 1, 0, vector_tokens, nc.vector.tensor_copy)
                if (s, t) == (1, 1):
                    quantize_x(1, 0)
                    quantize_x(1, 1)
                if (s, t) == (1, 2):
                    quantize_x(1, 2)
                if t == 1 and 2 <= s <= 5:
                    order_w_words(s // 2 + 1, 2 * (s % 2), 2)
                if t == 0 and s >= 2:
                    quantize_y(s - 2)
                    if s == LAST:
                        store_y_scales(0, GROUPS - 1)
            if s == LAST:
                for slot in range(SLOTS - 1):
                    for j in range(TILES):
                        turn_y(s, j, slot)
            clamp(s, SLOTS - 1)

        for j in range(TILES):
            turn_y(LAST, j, SLOTS - 1)
        quantize_y(LAST - 1)
        group_y(LAST, 0, SPAN, nc.vector.tensor_copy)
        for j in range(TILES - 1):
            store_y(LAST, j)
        quantize_y(LAST)
        store_y(LAST, TILES - 1)
        store_y_scales(GROUPS - 1, GROUPS)
